import numpy as np
import ml_dtypes


def mxq(x, axis, fmt="e4m3"):
    dtype, down = {"e4m3": (ml_dtypes.float8_e4m3fn, 7), "e5m2": (ml_dtypes.float8_e5m2, 14)}[fmt]
    v = np.moveaxis(np.asarray(x, np.float32).astype(ml_dtypes.bfloat16).astype(np.float64), axis, -1)
    blocks = v.reshape(v.shape[:-1] + (-1, 32))
    amax = np.abs(blocks).max(-1, keepdims=True)
    byte = np.maximum(np.where(amax > 0, np.frexp(amax)[1] - 1 + 127, 0) - down, 1)
    scale = np.exp2(byte - 127.0)
    codes = (blocks / scale).astype(np.float32).astype(dtype).astype(np.float64)
    return np.moveaxis((codes * scale).reshape(v.shape), -1, axis)


WIDE = False


def mx_kscale(k):
    if not WIDE:
        return np.ones(k)
    levels = np.array([10, -10, 5, -5, 0])
    if k % 512:
        return np.exp2(np.random.permutation(np.resize(levels, k // 32))).repeat(32)
    a = np.empty((k // 512, 16))
    for p in range(k // 512):
        a[p, :8] = np.random.permutation(np.resize(levels, 8))
        for g in range(8):
            far = levels[np.abs(levels - a[p, g]) >= 10]
            a[p, g + 8] = far[np.random.randint(len(far))]
    return np.exp2(a.ravel()).repeat(32)


def f64(x):
    return np.asarray(x).astype(np.float64)


def striped(idx):
    return np.tile(np.asarray(idx).reshape(-1, 16).T, (8, 1)).astype(np.uint16)


def unstriped(offs):
    return offs[:16].T.reshape(-1).astype(np.int64)


E2M1 = np.array([0.0, 0.5, 1.0, 1.5, 2.0, 3.0, 4.0, 6.0, -0.0, -0.5, -1.0, -1.5, -2.0, -3.0, -4.0, -6.0])


def pack_weight(w, fmt):
    k, n = w.shape
    w = f64(np.asarray(w, np.float32).astype(ml_dtypes.bfloat16)).reshape(k // 32, 32, n)
    amax = np.abs(w).max(1)
    if fmt == "e4m3":
        byte = np.frexp(amax)[1] - 1 + 127 - 7
    else:
        mant, ex = np.frexp(amax / 6.0)
        byte = np.where(mant > 0.5, ex, ex - 1) + 127
    byte = np.clip(np.where(amax > 0, byte, 1), 1, 254)
    scaled = (w * np.exp2(127.0 - byte)[:, None, :]).reshape(k, n).astype(np.float32)
    by_word = np.ascontiguousarray(scaled.reshape(k // 512, 128, 4, n).transpose(0, 1, 3, 2))
    if fmt == "e4m3":
        words = by_word.astype(ml_dtypes.float8_e4m3fn).view(np.uint8)
    else:
        c = by_word.astype(ml_dtypes.float4_e2m1fn).view(np.uint8) & 0xF
        words = (c[..., 0::2] | (c[..., 1::2] << 4)).reshape(k // 512, 128, 2 * n)
    return np.ascontiguousarray(words), np.ascontiguousarray(byte.astype(np.uint8).reshape(k // 512, 16, n))


def unpack_weight(words, scales, fmt):
    g, _, n = scales.shape
    words = np.ascontiguousarray(words).reshape(g, 128, n, -1)
    if fmt == "e4m3":
        vals = words.view(ml_dtypes.float8_e4m3fn).astype(np.float64)
    else:
        nib = np.empty((g, 128, n, 4), np.uint8)
        nib[..., 0::2] = words & 0xF
        nib[..., 1::2] = words >> 4
        vals = E2M1[nib]
    vals = vals * np.repeat(np.exp2(scales.astype(np.float64) - 127.0), 8, axis=1)[..., None]
    return vals.transpose(0, 1, 3, 2).reshape(g * 512, n)


def sigmoid(v):
    return 1.0 / (1.0 + np.exp(-v))


D, E, T, I, Q, G, B = 512, 512, 2048, 512, 128, 64, 8


def setup_inputs():
    n = np.random.standard_normal
    idx = np.random.permutation(T)[:I]
    fd = mx_kscale(D)
    fi = mx_kscale(I)
    ti = np.ones(T)
    ti[idx] = fi
    keysp = pack_weight(n((D, T)) / fd[:, None], "e4m3")
    return {
        "query": (n((D, Q)) * 0.8 / np.sqrt(D) * fd[:, None]).astype(np.float32),
        "keys_words": keysp[0],
        "keys_scales": keysp[1],
        "steep": (np.random.uniform(2.0, 8.0, (Q, 1))).astype(np.float32),
        "dquery": (n((D, Q)) * 0.6 / np.sqrt(D) * fd[:, None]).astype(np.float32),
        "os": (np.random.uniform(4.0, 16.0, (1, I)) * fi).astype(np.float32),
        "vals": (n((E, T)) / ti).astype(np.float32),
        "offs": striped(idx),
    }


def reference(query, keys_words, keys_scales, steep, dquery, os, vals, offs):
    idx = unstriped(offs)
    keysu = unpack_weight(keys_words, keys_scales, "e4m3")
    queryq = mxq(f64(query), 0, "e4m3")
    keysidxg = keysu[:, idx]
    a = queryq.T @ keysidxg
    dqueryq = mxq(f64(dquery), 0, "e4m3")
    ta = dqueryq.T @ keysidxg
    m1 = a.reshape(Q, G, I // G).mean(axis=2)
    m2 = m1.reshape(Q, B, G // B).mean(axis=2)
    mr = np.repeat(m2, G // B, axis=1)
    g1 = sigmoid((m1 - mr) * f64(steep))
    gr = np.repeat(g1, I // G, axis=1)
    p = np.exp(a) * gr
    z = np.sum(p, axis=1, keepdims=True)
    tm1 = ta.reshape(Q, G, I // G).mean(axis=2)
    tm2 = tm1.reshape(Q, B, G // B).mean(axis=2)
    tmr = np.repeat(tm2, G // B, axis=1)
    tg1 = (tm1 - tmr) * f64(steep) * g1 * (1.0 - g1)
    tgr = np.repeat(tg1, I // G, axis=1)
    tp = ta * np.exp(a) * gr + tgr * np.exp(a)
    tz = np.sum(tp, axis=1, keepdims=True)
    tw = (tp - tz * p / z) / z
    wo1 = tw * f64(os)
    wt1 = wo1.T
    vt1 = f64(vals)[:, idx].T
    wt1q = mxq(wt1, 0, "e4m3")
    vt1q = mxq(vt1, 0, "e4m3")
    o = wt1q.T @ vt1q
    return o

@@ -1,0 +1,236 @@
+import math
+from contextlib import ExitStack
+
+import concourse.mybir as mybir
+from concourse.masks import make_identity
+
+D, E, T, I, Q = 512, 512, 2048, 512, 128
+GROUP = 8
+N_GROUPS = I // GROUP
+BLOCK = 8
+N_BLOCKS = N_GROUPS // BLOCK
+P = 128
+PACK = 4
+E_TILES = E // P
+FLOPS = 2 * (2 * D * Q * I + I * Q * E)
+
+F32 = mybir.dt.float32
+BF16 = mybir.dt.bfloat16
+I32 = mybir.dt.int32
+U32 = mybir.dt.uint32
+U16 = mybir.dt.uint16
+U8 = mybir.dt.uint8
+FP8X4 = mybir.dt.float8_e4m3fn_x4
+ALU = mybir.AluOpType
+ACT = mybir.ActivationFunctionType
+AXIS_X = mybir.AxisListType.X
+
+SOFT = 8.0
+SHIFT_PER_BIT = SOFT * math.log(2.0) / 2.0**23
+SHIFT_OFFSET = SOFT * math.log(2.0) * (127 + 9)
+
+
+def tile_attend_ttblockcontrast_kernel(tc, query, keys_words, keys_scales, steep, dquery, slot_factor, vals, offs, out):
+    nc = tc.nc
+    with ExitStack() as ctx:
+        sb = ctx.enter_context(tc.tile_pool(name="sb", bufs=1))
+        ps = ctx.enter_context(tc.psum_pool(name="ps", bufs=1))
+
+        offsets = sb.tile([P, I // 16], U16, name="offsets")
+        key_pool = sb.tile([P, T], U32, name="key_pool", align_bytes=64)
+        scale_pool = sb.tile([P, T], U8, name="scale_pool", align_bytes=64)
+        q_raw = [sb.tile([P, PACK, Q], F32, name=f"q_raw{s}") for s in range(2)]
+        val_pool = [sb.tile([P, T], F32, name=f"val_pool{j}", tag=f"val_pool{j}", align_bytes=64) for j in range(E_TILES)]
+        steep_col = sb.tile([P, 1], F32, name="steep_col")
+        os_cols = sb.tile([P, PACK], F32, name="os_cols")
+
+        nc.gpsimd.memset(scale_pool[:].bitcast(I32), 0)
+        for raw, rows in zip(q_raw, (query, dquery)):
+            nc.sync.dma_start(out=raw[:], in_=rows.rearrange("(p t) q -> p t q", t=PACK))
+        nc.sync.dma_start(offsets[:], offs)
+        for quad in range(4):
+            nc.sync.dma_start(
+                out=scale_pool[32 * quad : 32 * quad + 4, :].bitcast(I32),
+                in_=keys_scales[0, 4 * quad : 4 * quad + 4, :].bitcast(I32),
+            )
+        nc.sync.dma_start(
+            out=key_pool[:].bitcast(I32), in_=keys_words[0].rearrange("p n t -> p (n t)").bitcast(I32)
+        )
+        nc.sync.dma_start(out=os_cols[:], in_=slot_factor.rearrange("o (p t) -> (o p) t", t=PACK))
+        nc.sync.dma_start(out=steep_col[:], in_=steep)
+        for j in range(E_TILES):
+            nc.sync.dma_start(out=val_pool[j][:], in_=vals[j * P : (j + 1) * P, :])
+
+        ident = sb.tile([P, P], F32, name="ident")
+        make_identity(nc, ident[:])
+
+        warm = sb.tile([P, 1], F32, name="warm")
+        nc.vector.memset(warm[:], 0.0)
+        warm_out = sb.tile([P, 1], F32, name="warm_out")
+        nc.scalar.activation(warm_out[:], warm[:], ACT.Exp)
+
+        half_slope = sb.tile([P, 1], F32, name="half_slope")
+        nc.gpsimd.tensor_scalar(half_slope[:], steep_col[:], 1.0 / (2 * GROUP), 0.0, ALU.mult, ALU.add)
+        neg_half_slope = sb.tile([P, 1], F32, name="neg_half_slope")
+        nc.gpsimd.tensor_scalar(neg_half_slope[:], steep_col[:], -1.0 / (2 * GROUP), 0.0, ALU.mult, ALU.add)
+
+        os_rows = ps.tile([P, PACK, P], F32, name="os_rows")
+        for t in range(PACK):
+            nc.tensor.transpose(os_rows[:, t, :], os_cols[:, t : t + 1].to_broadcast([P, P]), ident[:])
+
+
+        q_woven = sb.tile([P, 2, Q, PACK], BF16, name="q_woven", align_bytes=64)
+        for s in range(2):
+            nc.scalar.copy(
+                out=q_woven[:, s].rearrange("p (c i) t -> p c t i", i=4),
+                in_=q_raw[s][:].rearrange("p t (c i) -> p c t i", i=4),
+            )
+        q_codes = sb.tile([P, 2 * Q], U32, name="q_codes", align_bytes=64)
+        q_scales = sb.tile([P, 2 * Q], U8, name="q_scales", align_bytes=64)
+        key_scales = sb.tile([P, I], U8, name="key_scales", align_bytes=64)
+        nc.vector.tensor_copy(key_scales[:], scale_pool[:].indirect(offsets[:]))
+        nc.vector.quantize_mx(
+            out=q_codes[:].bitcast(FP8X4), scales=q_scales[:], in_=q_woven[:].rearrange("p s q t -> p (s q t)")
+        )
+
+        key_codes = sb.tile([P, I], U32, name="key_codes", align_bytes=64)
+        a = ps.tile([P, I], F32, name="a", tag="a")
+        ta = ps.tile([P, I], F32, name="ta", tag="ta")
+        for half in range(2):
+            slots = slice(half * I // 2, (half + 1) * I // 2)
+            entries = offsets[:, half * I // 32 : (half + 1) * I // 32]
+            nc.vector.tensor_copy(key_codes[:, slots], key_pool[:].indirect(entries))
+            for s, bank in enumerate((a, ta)):
+                rows = slice(s * Q, (s + 1) * Q)
+                nc.tensor.matmul_mx(
+                    out=bank[:, slots], lhsT=q_codes[:, rows].bitcast(FP8X4), lhsT_scale=q_scales[:, rows],
+                    rhs=key_codes[:, slots].bitcast(FP8X4), rhs_scale=key_scales[:, slots], start=True, stop=True,
+                )
+
+        def by_group(ap):
+            return ap.rearrange("p (g j) -> p g j", j=GROUP)
+
+        def spread(ap, n):
+            return ap.unsqueeze(2).to_broadcast([P, ap.shape[1], n])
+
+        def by_block(ap):
+            return ap.rearrange("p (b g) -> p b g", g=BLOCK)
+
+        def group_sums(bank, name):
+            sums = sb.tile([P, N_GROUPS], F32, name=name)
+            nc.vector.tensor_reduce(sums[:], by_group(bank[:]), AXIS_X, ALU.add)
+            return sums
+
+        def block_sums(sums, name):
+            totals = sb.tile([P, N_BLOCKS], F32, name=name)
+            nc.vector.tensor_reduce(totals[:], by_block(sums[:]), AXIS_X, ALU.add)
+            return totals
+
+        def contrast(sums, totals, name):
+            diff = sb.tile([P, N_GROUPS], F32, name=name, tag=name, align_bytes=64)
+            nc.vector.scalar_tensor_tensor(
+                by_block(diff[:]), spread(totals[:], BLOCK), -1.0 / BLOCK, by_block(sums[:]), ALU.mult, ALU.add
+            )
+            return diff
+
+        def gather_values(j, tag):
+            picked = sb.tile([P, I], BF16, name=f"picked{j}", tag=tag, align_bytes=64)
+            nc.vector.tensor_copy(picked[:], val_pool[j][:].indirect(offsets[:]))
+            return picked
+
+        def turn(rows, bank_tag, woven):
+            pairs = rows[:].bitcast(F32)
+            turned = ps.tile([P, 2, P], F32, name="turned", tag=bank_tag)
+            for u in range(2):
+                nc.tensor.transpose(turned[:, u, :], pairs[:, u : I // 2 : 2], ident[:])
+            nc.scalar.copy(out=woven, in_=turned[:].rearrange("p u r -> p r u"))
+
+        def quantise_turned(woven, name, tag):
+            width = woven.shape[1]
+            codes = sb.tile([P, width], U32, name=f"{name}_codes", tag=tag, align_bytes=64)
+            scales = sb.tile([P, width], U8, name=f"{name}_scales", align_bytes=64)
+            nc.vector.quantize_mx(
+                out=codes[:].bitcast(FP8X4), scales=scales[:],
+                in_=woven[:].rearrange("p r u -> p (r u)").bitcast(BF16),
+            )
+            return codes, scales
+
+        ex = sb.tile([P, I], F32, name="ex")
+        soft_sum = sb.tile([P, 1], F32, name="soft_sum", tag="soft_sum", align_bytes=64)
+        nc.scalar.activation(ex[:], a[:], ACT.Exp, scale=1.0 / SOFT, accum_out=soft_sum[:])
+        a_sums = group_sums(a, "a_sums")
+        ta_sums = group_sums(ta, "ta_sums")
+        a_totals = block_sums(a_sums, "a_totals")
+        neg_shift = sb.tile([P, 1], F32, name="neg_shift")
+        nc.vector.tensor_scalar(
+            neg_shift[:], soft_sum[:].bitcast(I32), -SHIFT_PER_BIT, SHIFT_OFFSET, ALU.mult, ALU.add
+        )
+        nc.scalar.activation(ex[:], a[:], ACT.Exp, bias=neg_shift[:])
+        ta_totals = block_sums(ta_sums, "ta_totals")
+        a_diff = contrast(a_sums, a_totals, "a_diff")
+        th = sb.tile([P, N_GROUPS], F32, name="th")
+        nc.scalar.activation(th[:], a_diff[:], ACT.Tanh, scale=half_slope[:])
+
+        woven_w0 = sb.tile([P, 2 * P, 2], F32, name="woven_w0", align_bytes=64)
+        woven12 = sb.tile([P, 2 * P, 2], F32, name="woven12", tag="woven12", align_bytes=64)
+        woven3 = sb.tile([P, P, 2], F32, name="woven3", align_bytes=64)
+        turn(gather_values(0, "soft_sum"), "v0_bank", woven_w0[:, P:, :])
+
+        rounded = sb.tile([P, T], BF16, name="rounded", tag="a_diff", align_bytes=64)
+        nc.scalar.activation(rounded[:], val_pool[1][:], ACT.Copy)
+        picked1 = sb.tile([P, I], BF16, name="picked1", align_bytes=64)
+        nc.scalar.activation(picked1[:], rounded[:].indirect(offsets[:]), ACT.Copy)
+
+        ta_diff = contrast(ta_sums, ta_totals, "ta_diff")
+        p2 = sb.tile([P, I], F32, name="p2")
+        z2 = sb.tile([P, 1], F32, name="z2")
+        nc.vector.scalar_tensor_tensor(
+            by_group(p2[:]), spread(th[:], GROUP), 1.0, by_group(ex[:]), ALU.add, ALU.mult, accum_out=z2[:]
+        )
+        gate_turn = sb.tile([P, N_GROUPS], F32, name="gate_turn", tag="gate_turn", align_bytes=64)
+        nc.vector.scalar_tensor_tensor(gate_turn[:], th[:], 1.0, ta_diff[:], ALU.subtract, ALU.mult)
+        rz = sb.tile([P, 1], F32, name="rz")
+        nc.vector.reciprocal(rz[:], z2[:])
+        rate = sb.tile([P, I], F32, name="rate", tag="rate", align_bytes=64)
+        nc.vector.scalar_tensor_tensor(
+            by_group(rate[:]), spread(gate_turn[:], GROUP), neg_half_slope[:], by_group(ta[:]), ALU.mult, ALU.add
+        )
+        p_os = sb.tile([P, I], F32, name="p_os", tag="p_os", align_bytes=64)
+        nc.vector.scalar_tensor_tensor(
+            p_os[:].rearrange("p (n t) -> p n t", t=PACK), p2[:].rearrange("p (n t) -> p n t", t=PACK), rz[:],
+            os_rows[:].rearrange("p t n -> p n t"), ALU.mult, ALU.mult,
+        )
+        weighted_rate = sb.tile([P, I], F32, name="weighted_rate")
+        mean_rate = sb.tile([P, 1], F32, name="mean_rate")
+        nc.vector.scalar_tensor_tensor(
+            weighted_rate[:], p2[:], rz[:], rate[:], ALU.mult, ALU.mult, accum_out=mean_rate[:]
+        )
+        turn(gather_values(2, "gate_turn"), "a", woven12[:, P:, :])
+        w = sb.tile([P, I], BF16, name="w", align_bytes=64)
+        nc.vector.scalar_tensor_tensor(w[:], rate[:], mean_rate[:], p_os[:], ALU.subtract, ALU.mult)
+
+        turn(picked1, "v1_bank", woven12[:, :P, :])
+        turn(w, "w_bank", woven_w0[:, :P, :])
+        turn(gather_values(3, "p_os"), "ta", woven3[:])
+
+        v12_codes, v12_scales = quantise_turned(woven12, "v12", "val_pool3")
+        w0_codes, w0_scales = quantise_turned(woven_w0, "w0", "woven12")
+        v3_codes, v3_scales = quantise_turned(woven3, "v3", "v3_codes")
+
+        def read_values(acc, codes, scales):
+            nc.tensor.matmul_mx(
+                out=acc, lhsT=w0_codes[:, :P].bitcast(FP8X4), lhsT_scale=w0_scales[:, :P],
+                rhs=codes.bitcast(FP8X4), rhs_scale=scales, start=True, stop=True,
+            )
+
+        early = ps.tile([P, 3 * P], F32, name="early")
+        read_values(early[:, :P], w0_codes[:, P:], w0_scales[:, P:])
+        read_values(early[:, P:], v12_codes[:], v12_scales[:])
+        last = ps.tile([P, P], F32, name="last")
+        read_values(last[:], v3_codes[:], v3_scales[:])
+        early_out = sb.tile([P, 3 * P], F32, name="early_out")
+        nc.scalar.copy(out=early_out[:], in_=early[:])
+        nc.sync.dma_start(out=out[:, : 3 * P], in_=early_out[:])
+        last_out = sb.tile([P, P], F32, name="last_out")
+        nc.vector.tensor_copy(out=last_out[:], in_=last[:])
+        nc.sync.dma_start(out=out[:, 3 * P :], in_=last_out[:])

@@ -44,20 +44,21 @@ def tile_attend_ttblockcontrast_kernel(tc, query, keys_words, keys_scales, steep
         steep_col = sb.tile([P, 1], F32, name="steep_col")
         os_cols = sb.tile([P, PACK], F32, name="os_cols")
 
-        nc.gpsimd.memset(scale_pool[:].bitcast(I32), 0)
-        for raw, rows in zip(q_raw, (query, dquery)):
-            nc.sync.dma_start(out=raw[:], in_=rows.rearrange("(p t) q -> p t q", t=PACK))
+        nc.vector.memset(scale_pool[:, : T // 2].bitcast(I32), 0)
+        nc.gpsimd.memset(scale_pool[:, T // 2 :].bitcast(I32), 0)
+        nc.sync.dma_start(out=q_raw[0][:], in_=query.rearrange("(p t) q -> p t q", t=PACK))
         nc.sync.dma_start(offsets[:], offs)
-        for quad in range(4):
-            nc.sync.dma_start(
+        nc.sync.dma_start(out=steep_col[:], in_=steep)
+        for quad, queue in enumerate((nc.sync, nc.scalar, nc.sync, nc.scalar)):
+            queue.dma_start(
                 out=scale_pool[32 * quad : 32 * quad + 4, :].bitcast(I32),
                 in_=keys_scales[0, 4 * quad : 4 * quad + 4, :].bitcast(I32),
             )
         nc.sync.dma_start(
             out=key_pool[:].bitcast(I32), in_=keys_words[0].rearrange("p n t -> p (n t)").bitcast(I32)
         )
+        nc.sync.dma_start(out=q_raw[1][:], in_=dquery.rearrange("(p t) q -> p t q", t=PACK))
         nc.sync.dma_start(out=os_cols[:], in_=slot_factor.rearrange("o (p t) -> (o p) t", t=PACK))
-        nc.sync.dma_start(out=steep_col[:], in_=steep)
         for j in range(E_TILES):
             nc.sync.dma_start(out=val_pool[j][:], in_=vals[j * P : (j + 1) * P, :])
 
@@ -74,38 +75,38 @@ def tile_attend_ttblockcontrast_kernel(tc, query, keys_words, keys_scales, steep
         neg_half_slope = sb.tile([P, 1], F32, name="neg_half_slope")
         nc.gpsimd.tensor_scalar(neg_half_slope[:], steep_col[:], -1.0 / (2 * GROUP), 0.0, ALU.mult, ALU.add)
 
-        os_rows = ps.tile([P, PACK, P], F32, name="os_rows")
-        for t in range(PACK):
-            nc.tensor.transpose(os_rows[:, t, :], os_cols[:, t : t + 1].to_broadcast([P, P]), ident[:])
-
-
-        q_woven = sb.tile([P, 2, Q, PACK], BF16, name="q_woven", align_bytes=64)
-        for s in range(2):
-            nc.scalar.copy(
-                out=q_woven[:, s].rearrange("p (c i) t -> p c t i", i=4),
-                in_=q_raw[s][:].rearrange("p t (c i) -> p c t i", i=4),
+        def quantise_rows(raw, name, weave):
+            woven = sb.tile([P, Q, PACK], BF16, name=f"{name}_woven", align_bytes=64)
+            weave(
+                out=woven[:].rearrange("p (c i) t -> p c t i", i=4),
+                in_=raw[:].rearrange("p t (c i) -> p c t i", i=4),
             )
-        q_codes = sb.tile([P, 2 * Q], U32, name="q_codes", align_bytes=64)
-        q_scales = sb.tile([P, 2 * Q], U8, name="q_scales", align_bytes=64)
+            codes = sb.tile([P, Q], U32, name=f"{name}_codes", align_bytes=64)
+            scales = sb.tile([P, Q], U8, name=f"{name}_scales", align_bytes=64)
+            nc.vector.quantize_mx(
+                out=codes[:].bitcast(FP8X4), scales=scales[:], in_=woven[:].rearrange("p q t -> p (q t)")
+            )
+            return codes, scales
+
+        def score(bank, codes, scales, slots):
+            nc.tensor.matmul_mx(
+                out=bank[:], lhsT=codes[:].bitcast(FP8X4), lhsT_scale=scales[:],
+                rhs=key_codes[:, slots].bitcast(FP8X4), rhs_scale=key_scales[:, slots], start=True, stop=True,
+            )
+
         key_scales = sb.tile([P, I], U8, name="key_scales", align_bytes=64)
         nc.vector.tensor_copy(key_scales[:], scale_pool[:].indirect(offsets[:]))
-        nc.vector.quantize_mx(
-            out=q_codes[:].bitcast(FP8X4), scales=q_scales[:], in_=q_woven[:].rearrange("p s q t -> p (s q t)")
-        )
-
+        q_codes, q_scales = quantise_rows(q_raw[0], "q", nc.vector.tensor_copy)
         key_codes = sb.tile([P, I], U32, name="key_codes", align_bytes=64)
-        a = ps.tile([P, I], F32, name="a", tag="a")
-        ta = ps.tile([P, I], F32, name="ta", tag="ta")
-        for half in range(2):
+        a_halves = [ps.tile([P, I // 2], F32, name=f"a{half}", tag=f"a{half}") for half in range(2)]
+        for half, a in enumerate(a_halves):
             slots = slice(half * I // 2, (half + 1) * I // 2)
             entries = offsets[:, half * I // 32 : (half + 1) * I // 32]
             nc.vector.tensor_copy(key_codes[:, slots], key_pool[:].indirect(entries))
-            for s, bank in enumerate((a, ta)):
-                rows = slice(s * Q, (s + 1) * Q)
-                nc.tensor.matmul_mx(
-                    out=bank[:, slots], lhsT=q_codes[:, rows].bitcast(FP8X4), lhsT_scale=q_scales[:, rows],
-                    rhs=key_codes[:, slots].bitcast(FP8X4), rhs_scale=key_scales[:, slots], start=True, stop=True,
-                )
+            score(a, q_codes, q_scales, slots)
+        dq_codes, dq_scales = quantise_rows(q_raw[1], "dq", nc.scalar.copy)
+        ta = ps.tile([P, I], F32, name="ta", tag="ta")
+        score(ta, dq_codes, dq_scales, slice(0, I))
 
         def by_group(ap):
             return ap.rearrange("p (g j) -> p g j", j=GROUP)
@@ -116,10 +117,6 @@ def tile_attend_ttblockcontrast_kernel(tc, query, keys_words, keys_scales, steep
         def by_block(ap):
             return ap.rearrange("p (b g) -> p b g", g=BLOCK)
 
-        def group_sums(bank, name):
-            sums = sb.tile([P, N_GROUPS], F32, name=name)
-            nc.vector.tensor_reduce(sums[:], by_group(bank[:]), AXIS_X, ALU.add)
-            return sums
 
         def block_sums(sums, name):
             totals = sb.tile([P, N_BLOCKS], F32, name=name)
@@ -145,36 +142,47 @@ def tile_attend_ttblockcontrast_kernel(tc, query, keys_words, keys_scales, steep
                 nc.tensor.transpose(turned[:, u, :], pairs[:, u : I // 2 : 2], ident[:])
             nc.scalar.copy(out=woven, in_=turned[:].rearrange("p u r -> p r u"))
 
-        def quantise_turned(woven, name, tag):
-            width = woven.shape[1]
-            codes = sb.tile([P, width], U32, name=f"{name}_codes", tag=tag, align_bytes=64)
-            scales = sb.tile([P, width], U8, name=f"{name}_scales", align_bytes=64)
+        def quantise_turned(woven, codes, scales):
             nc.vector.quantize_mx(
-                out=codes[:].bitcast(FP8X4), scales=scales[:],
-                in_=woven[:].rearrange("p r u -> p (r u)").bitcast(BF16),
+                out=codes.bitcast(FP8X4), scales=scales, in_=woven[:].rearrange("p r u -> p (r u)").bitcast(BF16)
             )
-            return codes, scales
 
         ex = sb.tile([P, I], F32, name="ex")
+        soft_sums = sb.tile([P, 2], F32, name="soft_sums")
+        a_sums = sb.tile([P, N_GROUPS], F32, name="a_sums")
+        for half, a in enumerate(a_halves):
+            nc.scalar.activation(
+                ex[:, half * I // 2 : (half + 1) * I // 2], a[:], ACT.Exp, scale=1.0 / SOFT,
+                accum_out=soft_sums[:, half : half + 1],
+            )
+        nc.vector.tensor_reduce(a_sums[:, : N_GROUPS // 2], by_group(a_halves[0][:]), AXIS_X, ALU.add)
         soft_sum = sb.tile([P, 1], F32, name="soft_sum", tag="soft_sum", align_bytes=64)
-        nc.scalar.activation(ex[:], a[:], ACT.Exp, scale=1.0 / SOFT, accum_out=soft_sum[:])
-        a_sums = group_sums(a, "a_sums")
-        ta_sums = group_sums(ta, "ta_sums")
-        a_totals = block_sums(a_sums, "a_totals")
+        nc.vector.tensor_tensor(soft_sum[:], soft_sums[:, 0:1], soft_sums[:, 1:2], ALU.add)
+        nc.vector.tensor_reduce(a_sums[:, N_GROUPS // 2 :], by_group(a_halves[1][:]), AXIS_X, ALU.add)
         neg_shift = sb.tile([P, 1], F32, name="neg_shift")
         nc.vector.tensor_scalar(
             neg_shift[:], soft_sum[:].bitcast(I32), -SHIFT_PER_BIT, SHIFT_OFFSET, ALU.mult, ALU.add
         )
-        nc.scalar.activation(ex[:], a[:], ACT.Exp, bias=neg_shift[:])
+        ta_sums = sb.tile([P, N_GROUPS], F32, name="ta_sums")
+        nc.vector.tensor_reduce(ta_sums[:], by_group(ta[:]), AXIS_X, ALU.add)
+        a_totals = block_sums(a_sums, "a_totals")
         ta_totals = block_sums(ta_sums, "ta_totals")
         a_diff = contrast(a_sums, a_totals, "a_diff")
+        for half, a in enumerate(a_halves):
+            nc.scalar.activation(ex[:, half * I // 2 : (half + 1) * I // 2], a[:], ACT.Exp, bias=neg_shift[:])
         th = sb.tile([P, N_GROUPS], F32, name="th")
         nc.scalar.activation(th[:], a_diff[:], ACT.Tanh, scale=half_slope[:])
+
+        os_rows = ps.tile([P, PACK, P], F32, name="os_rows", tag="a0")
+        for t in range(PACK):
+            nc.tensor.transpose(os_rows[:, t, :], os_cols[:, t : t + 1].to_broadcast([P, P]), ident[:])
+
 
         woven_w0 = sb.tile([P, 2 * P, 2], F32, name="woven_w0", align_bytes=64)
         woven12 = sb.tile([P, 2 * P, 2], F32, name="woven12", tag="woven12", align_bytes=64)
         woven3 = sb.tile([P, P, 2], F32, name="woven3", align_bytes=64)
-        turn(gather_values(0, "soft_sum"), "v0_bank", woven_w0[:, P:, :])
+        picked0 = sb.tile([P, I], BF16, name="picked0", tag="soft_sum", align_bytes=64)
+        nc.vector.tensor_copy(picked0[:, : I // 2], val_pool[0][:].indirect(offsets[:, : I // 32]))
 
         rounded = sb.tile([P, T], BF16, name="rounded", tag="a_diff", align_bytes=64)
         nc.scalar.activation(rounded[:], val_pool[1][:], ACT.Copy)
@@ -187,13 +195,13 @@ def tile_attend_ttblockcontrast_kernel(tc, query, keys_words, keys_scales, steep
         nc.vector.scalar_tensor_tensor(
             by_group(p2[:]), spread(th[:], GROUP), 1.0, by_group(ex[:]), ALU.add, ALU.mult, accum_out=z2[:]
         )
-        gate_turn = sb.tile([P, N_GROUPS], F32, name="gate_turn", tag="gate_turn", align_bytes=64)
-        nc.vector.scalar_tensor_tensor(gate_turn[:], th[:], 1.0, ta_diff[:], ALU.subtract, ALU.mult)
+        gate_turn = picked0[:, I // 2 : I // 2 + 2 * N_GROUPS].bitcast(F32)
+        nc.vector.scalar_tensor_tensor(gate_turn, th[:], 1.0, ta_diff[:], ALU.subtract, ALU.mult)
         rz = sb.tile([P, 1], F32, name="rz")
         nc.vector.reciprocal(rz[:], z2[:])
         rate = sb.tile([P, I], F32, name="rate", tag="rate", align_bytes=64)
         nc.vector.scalar_tensor_tensor(
-            by_group(rate[:]), spread(gate_turn[:], GROUP), neg_half_slope[:], by_group(ta[:]), ALU.mult, ALU.add
+            by_group(rate[:]), spread(gate_turn, GROUP), neg_half_slope[:], by_group(ta[:]), ALU.mult, ALU.add
         )
         p_os = sb.tile([P, I], F32, name="p_os", tag="p_os", align_bytes=64)
         nc.vector.scalar_tensor_tensor(
@@ -205,32 +213,36 @@ def tile_attend_ttblockcontrast_kernel(tc, query, keys_words, keys_scales, steep
         nc.vector.scalar_tensor_tensor(
             weighted_rate[:], p2[:], rz[:], rate[:], ALU.mult, ALU.mult, accum_out=mean_rate[:]
         )
-        turn(gather_values(2, "gate_turn"), "a", woven12[:, P:, :])
+        nc.vector.tensor_copy(picked0[:, I // 2 :], val_pool[0][:].indirect(offsets[:, I // 32 :]))
         w = sb.tile([P, I], BF16, name="w", align_bytes=64)
         nc.vector.scalar_tensor_tensor(w[:], rate[:], mean_rate[:], p_os[:], ALU.subtract, ALU.mult)
 
+        turn(picked0, "v0_bank", woven_w0[:, P:, :])
         turn(picked1, "v1_bank", woven12[:, :P, :])
         turn(w, "w_bank", woven_w0[:, :P, :])
+        turn(gather_values(2, "ta_diff"), "a1", woven12[:, P:, :])
         turn(gather_values(3, "p_os"), "ta", woven3[:])
 
-        v12_codes, v12_scales = quantise_turned(woven12, "v12", "val_pool3")
-        w0_codes, w0_scales = quantise_turned(woven_w0, "w0", "woven12")
-        v3_codes, v3_scales = quantise_turned(woven3, "v3", "v3_codes")
+        codes = sb.tile([P, 4 * P], U32, name="codes", tag="val_pool3", align_bytes=64)
+        scales = sb.tile([P, 4 * P], U8, name="scales", align_bytes=64)
+        codes3 = sb.tile([P, P], U32, name="codes3", align_bytes=64)
+        scales3 = sb.tile([P, P], U8, name="scales3", align_bytes=64)
+        quantise_turned(woven_w0, codes[:, : 2 * P], scales[:, : 2 * P])
+        quantise_turned(woven12, codes[:, 2 * P :], scales[:, 2 * P :])
+        quantise_turned(woven3, codes3[:], scales3[:])
 
-        def read_values(acc, codes, scales):
+        parts = (
+            (0, codes[:, P : 2 * P], scales[:, P : 2 * P], "v0_bank", nc.vector.tensor_copy),
+            (P, codes[:, 2 * P :], scales[:, 2 * P :], "out12", nc.scalar.copy),
+            (3 * P, codes3[:], scales3[:], "out3", nc.vector.tensor_copy),
+        )
+        for first, v_codes, v_scales, bank_tag, copy_out in parts:
+            width = v_codes.shape[1]
+            acc = ps.tile([P, width], F32, name="acc", tag=bank_tag)
             nc.tensor.matmul_mx(
-                out=acc, lhsT=w0_codes[:, :P].bitcast(FP8X4), lhsT_scale=w0_scales[:, :P],
-                rhs=codes.bitcast(FP8X4), rhs_scale=scales, start=True, stop=True,
+                out=acc[:], lhsT=codes[:, :P].bitcast(FP8X4), lhsT_scale=scales[:, :P],
+                rhs=v_codes.bitcast(FP8X4), rhs_scale=v_scales, start=True, stop=True,
             )
-
-        early = ps.tile([P, 3 * P], F32, name="early")
-        read_values(early[:, :P], w0_codes[:, P:], w0_scales[:, P:])
-        read_values(early[:, P:], v12_codes[:], v12_scales[:])
-        last = ps.tile([P, P], F32, name="last")
-        read_values(last[:], v3_codes[:], v3_scales[:])
-        early_out = sb.tile([P, 3 * P], F32, name="early_out")
-        nc.scalar.copy(out=early_out[:], in_=early[:])
-        nc.sync.dma_start(out=out[:, : 3 * P], in_=early_out[:])
-        last_out = sb.tile([P, P], F32, name="last_out")
-        nc.vector.tensor_copy(out=last_out[:], in_=last[:])
-        nc.sync.dma_start(out=out[:, 3 * P :], in_=last_out[:])
+            result = sb.tile([P, width], F32, name=f"result{first}")
+            copy_out(out=result[:], in_=acc[:])
+            nc.sync.dma_start(out=out[:, first : first + width], in_=result[:])

@@ -6,12 +6,14 @@ from concourse.masks import make_identity
 
 D, E, T, I, Q = 512, 512, 2048, 512, 128
 GROUP = 8
-N_GROUPS = I // GROUP
 BLOCK = 8
+N_GROUPS = I // GROUP
 N_BLOCKS = N_GROUPS // BLOCK
 P = 128
 PACK = 4
 E_TILES = E // P
+HALF = I // 2
+HALF_COLUMNS = HALF // 16
 FLOPS = 2 * (2 * D * Q * I + I * Q * E)
 
 F32 = mybir.dt.float32
@@ -46,6 +48,7 @@ def tile_attend_ttblockcontrast_kernel(tc, query, keys_words, keys_scales, steep
 
         nc.vector.memset(scale_pool[:, : T // 2].bitcast(I32), 0)
         nc.gpsimd.memset(scale_pool[:, T // 2 :].bitcast(I32), 0)
+
         nc.sync.dma_start(out=q_raw[0][:], in_=query.rearrange("(p t) q -> p t q", t=PACK))
         nc.sync.dma_start(offsets[:], offs)
         nc.sync.dma_start(out=steep_col[:], in_=steep)
@@ -65,15 +68,10 @@ def tile_attend_ttblockcontrast_kernel(tc, query, keys_words, keys_scales, steep
         ident = sb.tile([P, P], F32, name="ident")
         make_identity(nc, ident[:])
 
-        warm = sb.tile([P, 1], F32, name="warm")
-        nc.vector.memset(warm[:], 0.0)
-        warm_out = sb.tile([P, 1], F32, name="warm_out")
-        nc.scalar.activation(warm_out[:], warm[:], ACT.Exp)
-
         half_slope = sb.tile([P, 1], F32, name="half_slope")
-        nc.gpsimd.tensor_scalar(half_slope[:], steep_col[:], 1.0 / (2 * GROUP), 0.0, ALU.mult, ALU.add)
+        nc.scalar.activation(half_slope[:], steep_col[:], ACT.Copy, scale=1.0 / (2 * GROUP))
         neg_half_slope = sb.tile([P, 1], F32, name="neg_half_slope")
-        nc.gpsimd.tensor_scalar(neg_half_slope[:], steep_col[:], -1.0 / (2 * GROUP), 0.0, ALU.mult, ALU.add)
+        nc.scalar.activation(neg_half_slope[:], steep_col[:], ACT.Copy, scale=-1.0 / (2 * GROUP))
 
         def quantise_rows(raw, name, weave):
             woven = sb.tile([P, Q, PACK], BF16, name=f"{name}_woven", align_bytes=64)
@@ -81,16 +79,16 @@ def tile_attend_ttblockcontrast_kernel(tc, query, keys_words, keys_scales, steep
                 out=woven[:].rearrange("p (c i) t -> p c t i", i=4),
                 in_=raw[:].rearrange("p t (c i) -> p c t i", i=4),
             )
-            codes = sb.tile([P, Q], U32, name=f"{name}_codes", align_bytes=64)
-            scales = sb.tile([P, Q], U8, name=f"{name}_scales", align_bytes=64)
+            row_codes = sb.tile([P, Q], U32, name=f"{name}_codes", align_bytes=64)
+            row_scales = sb.tile([P, Q], U8, name=f"{name}_scales", align_bytes=64)
             nc.vector.quantize_mx(
-                out=codes[:].bitcast(FP8X4), scales=scales[:], in_=woven[:].rearrange("p q t -> p (q t)")
+                out=row_codes[:].bitcast(FP8X4), scales=row_scales[:], in_=woven[:].rearrange("p q t -> p (q t)")
             )
-            return codes, scales
+            return row_codes, row_scales
 
-        def score(bank, codes, scales, slots):
+        def score(bank, row_codes, row_scales, slots):
             nc.tensor.matmul_mx(
-                out=bank[:], lhsT=codes[:].bitcast(FP8X4), lhsT_scale=scales[:],
+                out=bank[:], lhsT=row_codes[:].bitcast(FP8X4), lhsT_scale=row_scales[:],
                 rhs=key_codes[:, slots].bitcast(FP8X4), rhs_scale=key_scales[:, slots], start=True, stop=True,
             )
 
@@ -98,10 +96,10 @@ def tile_attend_ttblockcontrast_kernel(tc, query, keys_words, keys_scales, steep
         nc.vector.tensor_copy(key_scales[:], scale_pool[:].indirect(offsets[:]))
         q_codes, q_scales = quantise_rows(q_raw[0], "q", nc.vector.tensor_copy)
         key_codes = sb.tile([P, I], U32, name="key_codes", align_bytes=64)
-        a_halves = [ps.tile([P, I // 2], F32, name=f"a{half}", tag=f"a{half}") for half in range(2)]
-        for half, a in enumerate(a_halves):
-            slots = slice(half * I // 2, (half + 1) * I // 2)
-            entries = offsets[:, half * I // 32 : (half + 1) * I // 32]
+        slot_halves = (slice(0, HALF), slice(HALF, I))
+        list_halves = (offsets[:, :HALF_COLUMNS], offsets[:, HALF_COLUMNS:])
+        a_halves = [ps.tile([P, HALF], F32, name=f"a{half}", tag=f"a{half}") for half in range(2)]
+        for a, slots, entries in zip(a_halves, slot_halves, list_halves):
             nc.vector.tensor_copy(key_codes[:, slots], key_pool[:].indirect(entries))
             score(a, q_codes, q_scales, slots)
         dq_codes, dq_scales = quantise_rows(q_raw[1], "dq", nc.scalar.copy)
@@ -111,12 +109,11 @@ def tile_attend_ttblockcontrast_kernel(tc, query, keys_words, keys_scales, steep
         def by_group(ap):
             return ap.rearrange("p (g j) -> p g j", j=GROUP)
 
-        def spread(ap, n):
-            return ap.unsqueeze(2).to_broadcast([P, ap.shape[1], n])
-
         def by_block(ap):
             return ap.rearrange("p (b g) -> p b g", g=BLOCK)
 
+        def spread(ap, n):
+            return ap.unsqueeze(2).to_broadcast([P, ap.shape[1], n])
 
         def block_sums(sums, name):
             totals = sb.tile([P, N_BLOCKS], F32, name=name)
@@ -139,21 +136,21 @@ def tile_attend_ttblockcontrast_kernel(tc, query, keys_words, keys_scales, steep
             pairs = rows[:].bitcast(F32)
             turned = ps.tile([P, 2, P], F32, name="turned", tag=bank_tag)
             for u in range(2):
-                nc.tensor.transpose(turned[:, u, :], pairs[:, u : I // 2 : 2], ident[:])
+                nc.tensor.transpose(turned[:, u, :], pairs[:, u:HALF:2], ident[:])
             nc.scalar.copy(out=woven, in_=turned[:].rearrange("p u r -> p r u"))
 
-        def quantise_turned(woven, codes, scales):
+        def quantise_turned(woven, turned_codes, turned_scales):
             nc.vector.quantize_mx(
-                out=codes.bitcast(FP8X4), scales=scales, in_=woven[:].rearrange("p r u -> p (r u)").bitcast(BF16)
+                out=turned_codes.bitcast(FP8X4), scales=turned_scales,
+                in_=woven[:].rearrange("p r u -> p (r u)").bitcast(BF16),
             )
 
         ex = sb.tile([P, I], F32, name="ex")
         soft_sums = sb.tile([P, 2], F32, name="soft_sums")
         a_sums = sb.tile([P, N_GROUPS], F32, name="a_sums")
-        for half, a in enumerate(a_halves):
+        for half, (a, slots) in enumerate(zip(a_halves, slot_halves)):
             nc.scalar.activation(
-                ex[:, half * I // 2 : (half + 1) * I // 2], a[:], ACT.Exp, scale=1.0 / SOFT,
-                accum_out=soft_sums[:, half : half + 1],
+                ex[:, slots], a[:], ACT.Exp, scale=1.0 / SOFT, accum_out=soft_sums[:, half : half + 1]
             )
         nc.vector.tensor_reduce(a_sums[:, : N_GROUPS // 2], by_group(a_halves[0][:]), AXIS_X, ALU.add)
         soft_sum = sb.tile([P, 1], F32, name="soft_sum", tag="soft_sum", align_bytes=64)
@@ -168,8 +165,8 @@ def tile_attend_ttblockcontrast_kernel(tc, query, keys_words, keys_scales, steep
         a_totals = block_sums(a_sums, "a_totals")
         ta_totals = block_sums(ta_sums, "ta_totals")
         a_diff = contrast(a_sums, a_totals, "a_diff")
-        for half, a in enumerate(a_halves):
-            nc.scalar.activation(ex[:, half * I // 2 : (half + 1) * I // 2], a[:], ACT.Exp, bias=neg_shift[:])
+        for a, slots in zip(a_halves, slot_halves):
+            nc.scalar.activation(ex[:, slots], a[:], ACT.Exp, bias=neg_shift[:])
         th = sb.tile([P, N_GROUPS], F32, name="th")
         nc.scalar.activation(th[:], a_diff[:], ACT.Tanh, scale=half_slope[:])
 
@@ -177,12 +174,12 @@ def tile_attend_ttblockcontrast_kernel(tc, query, keys_words, keys_scales, steep
         for t in range(PACK):
             nc.tensor.transpose(os_rows[:, t, :], os_cols[:, t : t + 1].to_broadcast([P, P]), ident[:])
 
-
         woven_w0 = sb.tile([P, 2 * P, 2], F32, name="woven_w0", align_bytes=64)
-        woven12 = sb.tile([P, 2 * P, 2], F32, name="woven12", tag="woven12", align_bytes=64)
+        woven12 = sb.tile([P, 2 * P, 2], F32, name="woven12", align_bytes=64)
         woven3 = sb.tile([P, P, 2], F32, name="woven3", align_bytes=64)
+
         picked0 = sb.tile([P, I], BF16, name="picked0", tag="soft_sum", align_bytes=64)
-        nc.vector.tensor_copy(picked0[:, : I // 2], val_pool[0][:].indirect(offsets[:, : I // 32]))
+        nc.vector.tensor_copy(picked0[:, :HALF], val_pool[0][:].indirect(list_halves[0]))
 
         rounded = sb.tile([P, T], BF16, name="rounded", tag="a_diff", align_bytes=64)
         nc.scalar.activation(rounded[:], val_pool[1][:], ACT.Copy)
@@ -195,11 +192,11 @@ def tile_attend_ttblockcontrast_kernel(tc, query, keys_words, keys_scales, steep
         nc.vector.scalar_tensor_tensor(
             by_group(p2[:]), spread(th[:], GROUP), 1.0, by_group(ex[:]), ALU.add, ALU.mult, accum_out=z2[:]
         )
-        gate_turn = picked0[:, I // 2 : I // 2 + 2 * N_GROUPS].bitcast(F32)
+        gate_turn = picked0[:, HALF : HALF + 2 * N_GROUPS].bitcast(F32)
         nc.vector.scalar_tensor_tensor(gate_turn, th[:], 1.0, ta_diff[:], ALU.subtract, ALU.mult)
         rz = sb.tile([P, 1], F32, name="rz")
         nc.vector.reciprocal(rz[:], z2[:])
-        rate = sb.tile([P, I], F32, name="rate", tag="rate", align_bytes=64)
+        rate = sb.tile([P, I], F32, name="rate", align_bytes=64)
         nc.vector.scalar_tensor_tensor(
             by_group(rate[:]), spread(gate_turn, GROUP), neg_half_slope[:], by_group(ta[:]), ALU.mult, ALU.add
         )
@@ -213,7 +210,7 @@ def tile_attend_ttblockcontrast_kernel(tc, query, keys_words, keys_scales, steep
         nc.vector.scalar_tensor_tensor(
             weighted_rate[:], p2[:], rz[:], rate[:], ALU.mult, ALU.mult, accum_out=mean_rate[:]
         )
-        nc.vector.tensor_copy(picked0[:, I // 2 :], val_pool[0][:].indirect(offsets[:, I // 32 :]))
+        nc.vector.tensor_copy(picked0[:, HALF:], val_pool[0][:].indirect(list_halves[1]))
         w = sb.tile([P, I], BF16, name="w", align_bytes=64)
         nc.vector.scalar_tensor_tensor(w[:], rate[:], mean_rate[:], p_os[:], ALU.subtract, ALU.mult)
 

import math
from contextlib import ExitStack

import concourse.mybir as mybir
from concourse.masks import make_identity

D, E, T, I, Q = 512, 512, 2048, 512, 128
GROUP = 8
BLOCK = 8
N_GROUPS = I // GROUP
N_BLOCKS = N_GROUPS // BLOCK
P = 128
PACK = 4
E_TILES = E // P
HALF = I // 2
HALF_COLUMNS = HALF // 16
FLOPS = 2 * (2 * D * Q * I + I * Q * E)

F32 = mybir.dt.float32
BF16 = mybir.dt.bfloat16
I32 = mybir.dt.int32
U32 = mybir.dt.uint32
U16 = mybir.dt.uint16
U8 = mybir.dt.uint8
FP8X4 = mybir.dt.float8_e4m3fn_x4
ALU = mybir.AluOpType
ACT = mybir.ActivationFunctionType
AXIS_X = mybir.AxisListType.X

SOFT = 8.0
SHIFT_PER_BIT = SOFT * math.log(2.0) / 2.0**23
SHIFT_OFFSET = SOFT * math.log(2.0) * (127 + 9)


def tile_attend_ttblockcontrast_kernel(tc, query, keys_words, keys_scales, steep, dquery, slot_factor, vals, offs, out):
    nc = tc.nc
    with ExitStack() as ctx:
        sb = ctx.enter_context(tc.tile_pool(name="sb", bufs=1))
        ps = ctx.enter_context(tc.psum_pool(name="ps", bufs=1))

        offsets = sb.tile([P, I // 16], U16, name="offsets")
        key_pool = sb.tile([P, T], U32, name="key_pool", align_bytes=64)
        scale_pool = sb.tile([P, T], U8, name="scale_pool", align_bytes=64)
        q_raw = [sb.tile([P, PACK, Q], F32, name=f"q_raw{s}") for s in range(2)]
        val_pool = [sb.tile([P, T], F32, name=f"val_pool{j}", tag=f"val_pool{j}", align_bytes=64) for j in range(E_TILES)]
        steep_col = sb.tile([P, 1], F32, name="steep_col")
        os_cols = sb.tile([P, PACK], F32, name="os_cols")

        nc.vector.memset(scale_pool[:, : T // 2].bitcast(I32), 0)
        nc.gpsimd.memset(scale_pool[:, T // 2 :].bitcast(I32), 0)

        nc.sync.dma_start(out=q_raw[0][:], in_=query.rearrange("(p t) q -> p t q", t=PACK))
        nc.sync.dma_start(offsets[:], offs)
        nc.sync.dma_start(out=steep_col[:], in_=steep)
        for quad, queue in enumerate((nc.sync, nc.scalar, nc.sync, nc.scalar)):
            queue.dma_start(
                out=scale_pool[32 * quad : 32 * quad + 4, :].bitcast(I32),
                in_=keys_scales[0, 4 * quad : 4 * quad + 4, :].bitcast(I32),
            )
        nc.sync.dma_start(
            out=key_pool[:].bitcast(I32), in_=keys_words[0].rearrange("p n t -> p (n t)").bitcast(I32)
        )
        nc.sync.dma_start(out=q_raw[1][:], in_=dquery.rearrange("(p t) q -> p t q", t=PACK))
        nc.sync.dma_start(out=os_cols[:], in_=slot_factor.rearrange("o (p t) -> (o p) t", t=PACK))
        for j in range(E_TILES):
            nc.sync.dma_start(out=val_pool[j][:], in_=vals[j * P : (j + 1) * P, :])

        ident = sb.tile([P, P], F32, name="ident")
        make_identity(nc, ident[:])

        half_slope = sb.tile([P, 1], F32, name="half_slope")
        nc.scalar.activation(half_slope[:], steep_col[:], ACT.Copy, scale=1.0 / (2 * GROUP))
        neg_half_slope = sb.tile([P, 1], F32, name="neg_half_slope")
        nc.scalar.activation(neg_half_slope[:], steep_col[:], ACT.Copy, scale=-1.0 / (2 * GROUP))

        def quantise_rows(raw, name, weave):
            woven = sb.tile([P, Q, PACK], BF16, name=f"{name}_woven", align_bytes=64)
            weave(
                out=woven[:].rearrange("p (c i) t -> p c t i", i=4),
                in_=raw[:].rearrange("p t (c i) -> p c t i", i=4),
            )
            row_codes = sb.tile([P, Q], U32, name=f"{name}_codes", align_bytes=64)
            row_scales = sb.tile([P, Q], U8, name=f"{name}_scales", align_bytes=64)
            nc.vector.quantize_mx(
                out=row_codes[:].bitcast(FP8X4), scales=row_scales[:], in_=woven[:].rearrange("p q t -> p (q t)")
            )
            return row_codes, row_scales

        def score(bank, row_codes, row_scales, slots):
            nc.tensor.matmul_mx(
                out=bank[:], lhsT=row_codes[:].bitcast(FP8X4), lhsT_scale=row_scales[:],
                rhs=key_codes[:, slots].bitcast(FP8X4), rhs_scale=key_scales[:, slots], start=True, stop=True,
            )

        key_scales = sb.tile([P, I], U8, name="key_scales", align_bytes=64)
        nc.vector.tensor_copy(key_scales[:], scale_pool[:].indirect(offsets[:]))
        q_codes, q_scales = quantise_rows(q_raw[0], "q", nc.vector.tensor_copy)
        key_codes = sb.tile([P, I], U32, name="key_codes", align_bytes=64)
        slot_halves = (slice(0, HALF), slice(HALF, I))
        list_halves = (offsets[:, :HALF_COLUMNS], offsets[:, HALF_COLUMNS:])
        a_halves = [ps.tile([P, HALF], F32, name=f"a{half}", tag=f"a{half}") for half in range(2)]
        for a, slots, entries in zip(a_halves, slot_halves, list_halves):
            nc.vector.tensor_copy(key_codes[:, slots], key_pool[:].indirect(entries))
            score(a, q_codes, q_scales, slots)
        dq_codes, dq_scales = quantise_rows(q_raw[1], "dq", nc.scalar.copy)
        ta = ps.tile([P, I], F32, name="ta", tag="ta")
        score(ta, dq_codes, dq_scales, slice(0, I))

        def by_group(ap):
            return ap.rearrange("p (g j) -> p g j", j=GROUP)

        def by_block(ap):
            return ap.rearrange("p (b g) -> p b g", g=BLOCK)

        def spread(ap, n):
            return ap.unsqueeze(2).to_broadcast([P, ap.shape[1], n])

        def block_sums(sums, name):
            totals = sb.tile([P, N_BLOCKS], F32, name=name)
            nc.vector.tensor_reduce(totals[:], by_block(sums[:]), AXIS_X, ALU.add)
            return totals

        def contrast(sums, totals, name):
            diff = sb.tile([P, N_GROUPS], F32, name=name, tag=name, align_bytes=64)
            nc.vector.scalar_tensor_tensor(
                by_block(diff[:]), spread(totals[:], BLOCK), -1.0 / BLOCK, by_block(sums[:]), ALU.mult, ALU.add
            )
            return diff

        def gather_values(j, tag):
            picked = sb.tile([P, I], BF16, name=f"picked{j}", tag=tag, align_bytes=64)
            nc.vector.tensor_copy(picked[:], val_pool[j][:].indirect(offsets[:]))
            return picked

        def turn(rows, bank_tag, woven):
            pairs = rows[:].bitcast(F32)
            turned = ps.tile([P, 2, P], F32, name="turned", tag=bank_tag)
            for u in range(2):
                nc.tensor.transpose(turned[:, u, :], pairs[:, u:HALF:2], ident[:])
            nc.scalar.copy(out=woven, in_=turned[:].rearrange("p u r -> p r u"))

        def quantise_turned(woven, turned_codes, turned_scales):
            nc.vector.quantize_mx(
                out=turned_codes.bitcast(FP8X4), scales=turned_scales,
                in_=woven[:].rearrange("p r u -> p (r u)").bitcast(BF16),
            )

        ex = sb.tile([P, I], F32, name="ex")
        soft_sums = sb.tile([P, 2], F32, name="soft_sums")
        a_sums = sb.tile([P, N_GROUPS], F32, name="a_sums")
        for half, (a, slots) in enumerate(zip(a_halves, slot_halves)):
            nc.scalar.activation(
                ex[:, slots], a[:], ACT.Exp, scale=1.0 / SOFT, accum_out=soft_sums[:, half : half + 1]
            )
        nc.vector.tensor_reduce(a_sums[:, : N_GROUPS // 2], by_group(a_halves[0][:]), AXIS_X, ALU.add)
        soft_sum = sb.tile([P, 1], F32, name="soft_sum", tag="soft_sum", align_bytes=64)
        nc.vector.tensor_tensor(soft_sum[:], soft_sums[:, 0:1], soft_sums[:, 1:2], ALU.add)
        nc.vector.tensor_reduce(a_sums[:, N_GROUPS // 2 :], by_group(a_halves[1][:]), AXIS_X, ALU.add)
        neg_shift = sb.tile([P, 1], F32, name="neg_shift")
        nc.vector.tensor_scalar(
            neg_shift[:], soft_sum[:].bitcast(I32), -SHIFT_PER_BIT, SHIFT_OFFSET, ALU.mult, ALU.add
        )
        ta_sums = sb.tile([P, N_GROUPS], F32, name="ta_sums")
        nc.vector.tensor_reduce(ta_sums[:], by_group(ta[:]), AXIS_X, ALU.add)
        a_totals = block_sums(a_sums, "a_totals")
        ta_totals = block_sums(ta_sums, "ta_totals")
        a_diff = contrast(a_sums, a_totals, "a_diff")
        for a, slots in zip(a_halves, slot_halves):
            nc.scalar.activation(ex[:, slots], a[:], ACT.Exp, bias=neg_shift[:])
        th = sb.tile([P, N_GROUPS], F32, name="th")
        nc.scalar.activation(th[:], a_diff[:], ACT.Tanh, scale=half_slope[:])

        os_rows = ps.tile([P, PACK, P], F32, name="os_rows", tag="a0")
        for t in range(PACK):
            nc.tensor.transpose(os_rows[:, t, :], os_cols[:, t : t + 1].to_broadcast([P, P]), ident[:])

        woven_w0 = sb.tile([P, 2 * P, 2], F32, name="woven_w0", align_bytes=64)
        woven12 = sb.tile([P, 2 * P, 2], F32, name="woven12", align_bytes=64)
        woven3 = sb.tile([P, P, 2], F32, name="woven3", align_bytes=64)

        picked0 = sb.tile([P, I], BF16, name="picked0", tag="soft_sum", align_bytes=64)
        nc.vector.tensor_copy(picked0[:, :HALF], val_pool[0][:].indirect(list_halves[0]))

        rounded = sb.tile([P, T], BF16, name="rounded", tag="a_diff", align_bytes=64)
        nc.scalar.activation(rounded[:], val_pool[1][:], ACT.Copy)
        picked1 = sb.tile([P, I], BF16, name="picked1", align_bytes=64)
        nc.scalar.activation(picked1[:], rounded[:].indirect(offsets[:]), ACT.Copy)

        ta_diff = contrast(ta_sums, ta_totals, "ta_diff")
        p2 = sb.tile([P, I], F32, name="p2")
        z2 = sb.tile([P, 1], F32, name="z2")
        nc.vector.scalar_tensor_tensor(
            by_group(p2[:]), spread(th[:], GROUP), 1.0, by_group(ex[:]), ALU.add, ALU.mult, accum_out=z2[:]
        )
        gate_turn = picked0[:, HALF : HALF + 2 * N_GROUPS].bitcast(F32)
        nc.vector.scalar_tensor_tensor(gate_turn, th[:], 1.0, ta_diff[:], ALU.subtract, ALU.mult)
        rz = sb.tile([P, 1], F32, name="rz")
        nc.vector.reciprocal(rz[:], z2[:])
        rate = sb.tile([P, I], F32, name="rate", align_bytes=64)
        nc.vector.scalar_tensor_tensor(
            by_group(rate[:]), spread(gate_turn, GROUP), neg_half_slope[:], by_group(ta[:]), ALU.mult, ALU.add
        )
        p_os = sb.tile([P, I], F32, name="p_os", tag="p_os", align_bytes=64)
        nc.vector.scalar_tensor_tensor(
            p_os[:].rearrange("p (n t) -> p n t", t=PACK), p2[:].rearrange("p (n t) -> p n t", t=PACK), rz[:],
            os_rows[:].rearrange("p t n -> p n t"), ALU.mult, ALU.mult,
        )
        weighted_rate = sb.tile([P, I], F32, name="weighted_rate")
        mean_rate = sb.tile([P, 1], F32, name="mean_rate")
        nc.vector.scalar_tensor_tensor(
            weighted_rate[:], p2[:], rz[:], rate[:], ALU.mult, ALU.mult, accum_out=mean_rate[:]
        )
        nc.vector.tensor_copy(picked0[:, HALF:], val_pool[0][:].indirect(list_halves[1]))
        w = sb.tile([P, I], BF16, name="w", align_bytes=64)
        nc.vector.scalar_tensor_tensor(w[:], rate[:], mean_rate[:], p_os[:], ALU.subtract, ALU.mult)

        turn(picked0, "v0_bank", woven_w0[:, P:, :])
        turn(picked1, "v1_bank", woven12[:, :P, :])
        turn(w, "w_bank", woven_w0[:, :P, :])
        turn(gather_values(2, "ta_diff"), "a1", woven12[:, P:, :])
        turn(gather_values(3, "p_os"), "ta", woven3[:])

        codes = sb.tile([P, 4 * P], U32, name="codes", tag="val_pool3", align_bytes=64)
        scales = sb.tile([P, 4 * P], U8, name="scales", align_bytes=64)
        codes3 = sb.tile([P, P], U32, name="codes3", align_bytes=64)
        scales3 = sb.tile([P, P], U8, name="scales3", align_bytes=64)
        quantise_turned(woven_w0, codes[:, : 2 * P], scales[:, : 2 * P])
        quantise_turned(woven12, codes[:, 2 * P :], scales[:, 2 * P :])
        quantise_turned(woven3, codes3[:], scales3[:])

        parts = (
            (0, codes[:, P : 2 * P], scales[:, P : 2 * P], "v0_bank", nc.vector.tensor_copy),
            (P, codes[:, 2 * P :], scales[:, 2 * P :], "out12", nc.scalar.copy),
            (3 * P, codes3[:], scales3[:], "out3", nc.vector.tensor_copy),
        )
        for first, v_codes, v_scales, bank_tag, copy_out in parts:
            width = v_codes.shape[1]
            acc = ps.tile([P, width], F32, name="acc", tag=bank_tag)
            nc.tensor.matmul_mx(
                out=acc[:], lhsT=codes[:, :P].bitcast(FP8X4), lhsT_scale=scales[:, :P],
                rhs=v_codes.bitcast(FP8X4), rhs_scale=v_scales, start=True, stop=True,
            )
            result = sb.tile([P, width], F32, name=f"result{first}")
            copy_out(out=result[:], in_=acc[:])
            nc.sync.dma_start(out=out[:, first : first + width], in_=result[:])
